import numpy as np
import ml_dtypes


def mxq(x, axis, fmt="e4m3"):
    dtype, down = {"e4m3": (ml_dtypes.float8_e4m3fn, 7), "e5m2": (ml_dtypes.float8_e5m2, 14)}[fmt]
    v = np.moveaxis(np.asarray(x, np.float32).astype(ml_dtypes.bfloat16).astype(np.float64), axis, -1)
    blocks = v.reshape(v.shape[:-1] + (-1, 32))
    amax = np.abs(blocks).max(-1, keepdims=True)
    byte = np.maximum(np.where(amax > 0, np.frexp(amax)[1] - 1 + 127, 0) - down, 1)
    scale = np.exp2(byte - 127.0)
    codes = (blocks / scale).astype(np.float32).astype(dtype).astype(np.float64)
    return np.moveaxis((codes * scale).reshape(v.shape), -1, axis)


WIDE = False


def mx_kscale(k, group=512):
    if not WIDE:
        return np.ones(k)
    levels = np.array([10, -10, 5, -5, 0])
    if group != 512:
        return np.exp2(np.random.permutation(np.resize(levels, k // group))).repeat(group)
    if k % 512:
        return np.exp2(np.random.permutation(np.resize(levels, k // 32))).repeat(32)
    a = np.empty((k // 512, 16))
    for p in range(k // 512):
        a[p, :8] = np.random.permutation(np.resize(levels, 8))
        for g in range(8):
            far = levels[np.abs(levels - a[p, g]) >= 10]
            a[p, g + 8] = far[np.random.randint(len(far))]
    return np.exp2(a.ravel()).repeat(32)


def f64(x):
    return np.asarray(x).astype(np.float64)


def striped(idx):
    return np.tile(np.asarray(idx).reshape(-1, 16).T, (8, 1)).astype(np.uint16)


def unstriped(offs):
    return offs[:16].T.reshape(-1).astype(np.int64)


H, KV, D, NQ, N = 8, 8, 128, 512, 512


def setup_inputs():
    n = np.random.standard_normal
    s = mx_kscale(D, 0)[:, None]
    u = mx_kscale(N)
    t = np.random.uniform(0.5, 2.0, N) * u
    v = n((KV, N, 128))
    return {
        "qT": (n((H, D, NQ)) * s * (0.70 / np.sqrt(D))).astype(np.float32),
        "kT": (n((KV, D, N)) / s).astype(np.float32),
        "t": t.reshape(N, 1).astype(np.float32),
        "v": (v / t[:, None]).astype(np.float32),
    }


def reference(qT, kT, t, v):
    a = mxq(f64(kT), 1, "e4m3").transpose(0, 2, 1) @ mxq(f64(qT), 1, "e4m3")
    p = 1.0 / (1.0 + np.exp(-a))
    w = p * f64(t)
    y = mxq(w, 1, "e4m3").transpose(0, 2, 1) @ mxq(f64(v), 1, "e4m3")
    y = y / 16.0
    return y

from contextlib import ExitStack

import concourse.mybir as mybir

H, D, NQ, N, E = 8, 128, 512, 512, 128
FLOPS = 2 * H * N * NQ * D + 2 * H * NQ * N * E

F32 = mybir.dt.float32
BF16 = mybir.dt.bfloat16
U32 = mybir.dt.uint32
U8 = mybir.dt.uint8
FP8X4 = mybir.dt.float8_e4m3fn_x4
ACT = mybir.ActivationFunctionType
ALU = mybir.AluOpType

P = 128
PACK = 4
ROWS = 32
SIDE = 4
SETS = 2
QC = 128
CHUNKS = NQ // QC
HALF = N // 2
GROUPS = [1,1,2,4,4,4,4,4,2,2,2,1,1]


def tile_rows_a_sigmoid_kernel(tc, qT, kT, t, v, out):
    nc = tc.nc
    with ExitStack() as ctx:
        keep = ctx.enter_context(tc.tile_pool(name="keep", bufs=1))
        ring = ctx.enter_context(tc.tile_pool(name="ring", bufs=5))
        psum = ctx.enter_context(tc.psum_pool(name="psum", bufs=1))
        ctx.enter_context(tc.manual_schedule())

        def kept(name, shape, dtype):
            return keep.tile(shape, dtype, name=name, align_bytes=64)

        q_hbm = qT.rearrange("(s g) (p j) n -> s (g p) j n", g=SIDE, j=PACK)
        k_hbm = kT.rearrange("(s g) (p j) n -> s (g p) j n", g=SIDE, j=PACK)
        v_hbm = v.rearrange("(s g) (p j) e -> s p g (j e)", g=SIDE, j=PACK)

        t_sb = kept("t_sb", [P, PACK], F32)
        warm = kept("warm", [P, 8], F32)
        warm_out = kept("warm_out", [P, 8], F32)

        k_codes = [kept("k_codes%d" % s, [P, N], U32) for s in range(SETS)]
        k_scales = [kept("k_scales%d" % s, [P, N], U8) for s in range(SETS)]
        q_codes = [kept("q_codes%d" % s, [P, NQ], U32) for s in range(SETS)]
        q_scales = [kept("q_scales%d" % s, [P, NQ], U8) for s in range(SETS)]
        v_codes = [kept("v_codes%d" % s, [P, SIDE * E], U32) for s in range(SETS)]
        v_scales = [kept("v_scales%d" % s, [P, SIDE * E], U8) for s in range(SETS)]
        q_bf = [kept("q_bf%d" % s, [P, NQ * PACK], BF16) for s in range(SETS)]
        v_bf = [kept("v_bf%d" % s, [P, SIDE * E * PACK], BF16) for s in range(SETS)]
        score = [psum.tile([P, PACK, QC], F32, name="score%d" % g) for g in range(SIDE)]
        y_bank = [psum.tile([P, SIDE, E], F32, name="y_bank%d" % b) for b in range(4)]

        k_raw, k_bf, q_raw, v_raw = {}, {}, {}, {}
        p_sb, w_bf, w_codes, w_scales = {}, {}, {}, {}
        first = [sum(GROUPS[:i]) for i in range(len(GROUPS))]
        group_of = [i for i in range(len(GROUPS)) for b in range(GROUPS[i])]

        def copy(engine, dst, src):
            if engine == "V":
                nc.vector.tensor_copy(out=dst, in_=src)
            else:
                nc.scalar.copy(out=dst, in_=src)

        def quantize(codes, scales, src):
            nc.vector.quantize_mx(out=codes.bitcast(FP8X4), scales=scales, in_=src)

        def load_k(s, a):
            k_raw[s, a] = kept("k_raw%d_%d" % (s, a), [P, PACK, HALF], F32)
            nc.sync.dma_start(out=k_raw[s, a][:], in_=k_hbm[s, :, :, a * HALF : (a + 1) * HALF])

        def load_q(s, c0, c1):
            raw = kept("q_raw%d_%d" % (s, c0), [P, PACK, (c1 - c0) * QC], F32)
            nc.sync.dma_start(out=raw[:], in_=q_hbm[s, :, :, c0 * QC : c1 * QC])
            for c in range(c0, c1):
                q_raw[s, c] = (raw, c0)

        def load_v(s):
            v_raw[s] = kept("v_raw%d" % s, [P, SIDE, PACK * E], F32)
            nc.sync.dma_start(out=v_raw[s][:], in_=v_hbm[s])

        def cast_k(engine, s, a):
            k_bf[s, a] = kept("k_bf%d_%d" % (s, a), [P, PACK, HALF], BF16)
            copy(
                engine,
                k_bf[s, a][:].rearrange("p r (m j) -> p m j r", j=PACK),
                k_raw[s, a][:].rearrange("p j (m r) -> p m j r", r=PACK),
            )

        def quant_k(s, a):
            for r in range(PACK):
                cols = slice(r * P + a * 64, r * P + (a + 1) * 64)
                quantize(k_codes[s][:, cols], k_scales[s][:, cols], k_bf[s, a][:, r, :])

        def cast_q(engine, s, c0, c1):
            raw, base = q_raw[s, c0]
            copy(
                engine,
                q_bf[s][:, c0 * QC * PACK : c1 * QC * PACK].rearrange("p (m i j) -> p m j i", i=4, j=PACK),
                raw[:, :, (c0 - base) * QC : (c1 - base) * QC].rearrange("p j (m i) -> p m j i", i=4),
            )

        def quant_q(s, c0, c1):
            cols = slice(c0 * QC, c1 * QC)
            quantize(q_codes[s][:, cols], q_scales[s][:, cols], q_bf[s][:, c0 * QC * PACK : c1 * QC * PACK])

        def cast_v(engine, s, g0, g1):
            copy(
                engine,
                v_bf[s][:, g0 * E * PACK : g1 * E * PACK].rearrange("p (g m i j) -> p g m j i", m=E // 4, i=4, j=PACK),
                v_raw[s][:, g0:g1, :].rearrange("p g (j m i) -> p g m j i", j=PACK, i=4),
            )

        def quant_v(s, g0, g1):
            cols = slice(g0 * E, g1 * E)
            quantize(v_codes[s][:, cols], v_scales[s][:, cols], v_bf[s][:, g0 * E * PACK : g1 * E * PACK])

        def score_pass(n, r):
            s, c, g = n // 16, (n // SIDE) % CHUNKS, n % SIDE
            rows = slice(g * ROWS, (g + 1) * ROWS)
            keys = slice(r * P, (r + 1) * P)
            queries = slice(c * QC, (c + 1) * QC)
            nc.tensor.matmul_mx(
                out=score[g][:, r, :],
                lhsT=k_codes[s][rows, keys].bitcast(FP8X4),
                lhsT_scale=k_scales[s][rows, keys],
                rhs=q_codes[s][rows, queries].bitcast(FP8X4),
                rhs_scale=q_scales[s][rows, queries],
                start=True,
                stop=True,
            )

        def fill(n):
            for r in range(2):
                if n < 32:
                    score_pass(n, r)
                if SIDE < n <= 32:
                    score_pass(n - 1, 2 + r)

        def sig(n):
            i = group_of[n]
            if n == first[i]:
                p_sb[i] = ring.tile([P, GROUPS[i], QC, PACK], F32, name="p_sb", tag="p_sb", align_bytes=64)
            nc.scalar.activation(
                out=p_sb[i][:, n - first[i]],
                in_=score[n % SIDE][:].rearrange("p r q -> p q r"),
                func=ACT.Sigmoid,
            )
            fill(n + SIDE)

        def sigs(n0, n1):
            for n in range(n0, n1):
                sig(n)

        def tt(i):
            cols = GROUPS[i] * QC
            w_bf[i] = ring.tile([P, cols * PACK], BF16, name="w_bf", tag="w_bf", align_bytes=64)
            nc.vector.tensor_tensor(
                out=w_bf[i][:].rearrange("p (q r) -> p q r", r=PACK),
                in0=p_sb[i][:].rearrange("p b q r -> p (b q) r"),
                in1=t_sb[:].unsqueeze(1).to_broadcast([P, cols, PACK]),
                op=ALU.mult,
            )

        def qw(i):
            cols = GROUPS[i] * QC
            w_codes[i] = kept("w_codes%d" % i, [P, cols], U32)
            w_scales[i] = kept("w_scales%d" % i, [P, cols], U8)
            quantize(w_codes[i][:], w_scales[i][:], w_bf[i][:])

        def pv(i):
            s = first[i] // 16
            for b in range(GROUPS[i]):
                g = (first[i] + b) % SIDE
                queries = slice(b * QC, (b + 1) * QC)
                feats = slice(g * E, (g + 1) * E)
                nc.tensor.matmul_mx(
                    out=y_bank[i % 4][:, b, :],
                    lhsT=w_codes[i][:, queries].bitcast(FP8X4),
                    lhsT_scale=w_scales[i][:, queries],
                    rhs=v_codes[s][:, feats].bitcast(FP8X4),
                    rhs_scale=v_scales[s][:, feats],
                    start=True,
                    stop=True,
                )

        def ev(i, engine="S"):
            n, nb = first[i], GROUPS[i]
            s, c, g = n // 16, (n // SIDE) % CHUNKS, n % SIDE
            y_sb = kept("y_sb%d" % i, [P, nb, E], F32)
            if engine == "S":
                nc.scalar.mul(out=y_sb[:], in_=y_bank[i % 4][:, :nb, :], mul=1.0 / 16.0)
            else:
                nc.vector.tensor_scalar_mul(out=y_sb[:], in0=y_bank[i % 4][:, :nb, :], scalar1=1.0 / 16.0)
            h = s * SIDE + g
            nc.sync.dma_start(
                out=out[h : h + nb, c * QC : (c + 1) * QC, :].rearrange("g p e -> p g e"), in_=y_sb[:]
            )

        def setup():
            nc.vector.memset(warm[:], 0.0)
            nc.scalar.activation(out=warm_out[:], in_=warm[:], func=ACT.Sigmoid)

        def load_t():
            nc.sync.dma_start(out=t_sb[:], in_=t.rearrange("(p j) o -> p (j o)", j=PACK))

        def first_fill():
            for r in range(PACK):
                for n in range(SIDE):
                    score_pass(n, r)

        setup()
        load_k(0,0)
        load_k(0,1)
        load_q(0,0,1)
        load_t()
        load_q(0,1,2)
        load_q(0,2,4)
        load_k(1,0)
        load_k(1,1)
        load_q(1,0,4)
        load_v(0)
        load_v(1)
        cast_k("V",0,0)
        cast_k("V",0,1)
        cast_q("S",0,0,1)
        cast_q("S",0,1,2)
        quant_k(0,0)
        quant_k(0,1)
        quant_q(0,0,1)
        first_fill()
        quant_q(0,1,2)
        cast_q("V",0,2,4)
        sig(0)
        tt(0)
        quant_q(0,2,4)
        sig(1)
        tt(1)
        qw(0)
        sigs(2,4)
        tt(2)
        qw(1)
        cast_k("V",1,0)
        qw(2)
        cast_k("V",1,1)
        quant_k(1,0)
        sigs(4,8)
        tt(3)
        quant_k(1,1)
        sigs(8,10)
        cast_q("S",1,0,2)
        quant_q(1,0,2)
        sigs(10,12)
        qw(3)
        cast_v("V",0,0,4)
        tt(4)
        quant_v(0,0,4)
        cast_q("S",1,2,4)
        sigs(12,16)
        quant_q(1,2,4)
        qw(4)
        tt(5)
        cast_v("S",1,0,2)
        sigs(16,18)
        pv(0)
        pv(1)
        pv(2)
        pv(3)
        sigs(18,20)
        cast_v("S",1,2,4)
        ev(0)
        ev(1)
        ev(2)
        pv(4)
        quant_v(1,0,2)
        qw(5)
        tt(6)
        sigs(20,24)
        ev(3)
        pv(5)
        quant_v(1,2,4)
        qw(6)
        tt(7)
        sigs(24,26)
        ev(4)
        sigs(26,28)
        ev(5)
        pv(6)
        tt(8)
        qw(7)
        tt(9)
        qw(8)
        sigs(28,30)
        ev(6)
        pv(7)
        sigs(30,32)
        ev(7)
        pv(8)
        ev(8)
        tt(10)
        qw(9)
        pv(9)
        ev(9)
        tt(11)
        qw(10)
        pv(10)
        ev(10)
        tt(12)
        qw(11)
        pv(11)
        ev(11)
        qw(12)
        pv(12)
        ev(12)
